import numpy as np
import ml_dtypes

BF16 = ml_dtypes.bfloat16


def bf(x):
    return np.asarray(x, np.float32).astype(BF16)


def f32(x):
    return np.asarray(x, np.float32)


def f64(x):
    return np.asarray(x).astype(np.float64)


def striped(idx):
    return np.tile(idx.reshape(-1, 16).T, (8, 1))


S, K, M, N, E, Q, H = 256, 128, 256, 256, 2, 128, 128


def sigmoid(v):
    return 1.0 / (1.0 + np.exp(-v))


def setup_inputs():
    return {"table": bf(np.random.standard_normal((K, S))), "w": bf(np.random.standard_normal((E, K, M)) / np.sqrt(K)), "offs": striped(np.sort(np.random.permutation(S).reshape(E, Q), axis=1).reshape(-1))}


def reference(table, w, offs):
    idx = offs[:16].T.reshape(-1)
    x = f64(table)[:, idx]
    y = np.concatenate([f64(w)[e].T @ x[:, e * Q : (e + 1) * Q] for e in range(E)], axis=1)
    return y[:H] * sigmoid(y[H:])

@@ -1,0 +1,52 @@
+import concourse.mybir as mybir
+
+BF16, F32, U16 = mybir.dt.bfloat16, mybir.dt.float32, mybir.dt.uint16
+SIGMOID = mybir.ActivationFunctionType.Sigmoid
+MULT = mybir.AluOpType.mult
+
+K = 128
+S = 256
+E = 2
+Q = 128
+H = 128
+N = E * Q
+QC = Q // 16
+BANK = 512
+
+FLOPS = 2 * K * 2 * H * N
+
+
+def tile_gather_matmul_kernel(tc, table, w, offs, out):
+    nc = tc.nc
+    with (
+        tc.tile_pool(name="held", bufs=1) as held,
+        tc.psum_pool(name="psum", bufs=1) as psum,
+    ):
+        offsets = held.tile([128, N // 16], U16, name="offsets")
+        nc.sync.dma_start(offsets[:], offs)
+        tokens = held.tile([K, S], BF16, name="tokens")
+        nc.scalar.dma_start(tokens[:], table)
+        weights = [held.tile([K, 2 * H], BF16, name="weights%d" % e) for e in range(E)]
+        queues = (nc.sync, nc.scalar)
+        for e in range(E):
+            queues[e].dma_start(weights[e][:], w[e])
+
+        gates = [psum.tile([H, BANK], F32, name="gates%d" % e) for e in range(E)]
+        values = [psum.tile([H, BANK], F32, name="values%d" % e) for e in range(E)]
+        for banks, first in ((gates, H), (values, 0)):
+            for e in range(E):
+                picked = tokens[:].indirect(offsets[:, e * QC : (e + 1) * QC])
+                nc.tensor.matmul(
+                    banks[e][:, :Q],
+                    weights[e][:, first : first + H],
+                    picked,
+                    start=True,
+                    stop=True,
+                )
+
+        result = held.tile([H, N], F32, name="result")
+        for e in range(E):
+            opened = held.tile([H, Q], F32, name="opened%d" % e)
+            nc.scalar.activation(opened[:], gates[e][:, :Q], SIGMOID)
+            nc.vector.tensor_tensor(result[:, e * Q : (e + 1) * Q], values[e][:, :Q], opened[:], MULT)
+        nc.sync.dma_start(out, result[:])

@@ -44,9 +44,9 @@ def tile_gather_matmul_kernel(tc, table, w, offs, out):
                     stop=True,
                 )
 
-        result = held.tile([H, N], F32, name="result")
         for e in range(E):
             opened = held.tile([H, Q], F32, name="opened%d" % e)
             nc.scalar.activation(opened[:], gates[e][:, :Q], SIGMOID)
-            nc.vector.tensor_tensor(result[:, e * Q : (e + 1) * Q], values[e][:, :Q], opened[:], MULT)
-        nc.sync.dma_start(out, result[:])
+            result = held.tile([H, Q], F32, name="result%d" % e)
+            nc.vector.tensor_tensor(result[:], values[e][:, :Q], opened[:], MULT)
+            nc.sync.dma_start(out[:, e * Q : (e + 1) * Q], result[:])

@@ -12,6 +12,7 @@ H = 128
 N = E * Q
 QC = Q // 16
 BANK = 512
+ROW = 512
 
 FLOPS = 2 * K * 2 * H * N
 
@@ -24,9 +25,11 @@ def tile_gather_matmul_kernel(tc, table, w, offs, out):
     ):
         offsets = held.tile([128, N // 16], U16, name="offsets")
         nc.sync.dma_start(offsets[:], offs)
-        tokens = held.tile([K, S], BF16, name="tokens")
+        tokens = held.tile([K, S], BF16, name="tokens", align_bytes=ROW)
         nc.scalar.dma_start(tokens[:], table)
-        weights = [held.tile([K, 2 * H], BF16, name="weights%d" % e) for e in range(E)]
+        weights = [
+            held.tile([K, 2 * H], BF16, name="weights%d" % e, align_bytes=ROW) for e in range(E)
+        ]
         queues = (nc.sync, nc.scalar)
         for e in range(E):
             queues[e].dma_start(weights[e][:], w[e])
@@ -47,6 +50,6 @@ def tile_gather_matmul_kernel(tc, table, w, offs, out):
         for e in range(E):
             opened = held.tile([H, Q], F32, name="opened%d" % e)
             nc.scalar.activation(opened[:], gates[e][:, :Q], SIGMOID)
-            result = held.tile([H, Q], F32, name="result%d" % e)
+            result = held.tile([H, Q], F32, name="result%d" % e, align_bytes=ROW)
             nc.vector.tensor_tensor(result[:], values[e][:, :Q], opened[:], MULT)
             nc.sync.dma_start(out[:, e * Q : (e + 1) * Q], result[:])

import concourse.mybir as mybir

BF16, F32, U16 = mybir.dt.bfloat16, mybir.dt.float32, mybir.dt.uint16
SIGMOID = mybir.ActivationFunctionType.Sigmoid
MULT = mybir.AluOpType.mult

K = 128
S = 256
E = 2
Q = 128
H = 128
N = E * Q
QC = Q // 16
BANK = 512
ROW = 512

FLOPS = 2 * K * 2 * H * N


def tile_gather_matmul_kernel(tc, table, w, offs, out):
    nc = tc.nc
    with (
        tc.tile_pool(name="held", bufs=1) as held,
        tc.psum_pool(name="psum", bufs=1) as psum,
    ):
        offsets = held.tile([128, N // 16], U16, name="offsets")
        nc.sync.dma_start(offsets[:], offs)
        tokens = held.tile([K, S], BF16, name="tokens", align_bytes=ROW)
        nc.scalar.dma_start(tokens[:], table)
        weights = [
            held.tile([K, 2 * H], BF16, name="weights%d" % e, align_bytes=ROW) for e in range(E)
        ]
        queues = (nc.sync, nc.scalar)
        for e in range(E):
            queues[e].dma_start(weights[e][:], w[e])

        gates = [psum.tile([H, BANK], F32, name="gates%d" % e) for e in range(E)]
        values = [psum.tile([H, BANK], F32, name="values%d" % e) for e in range(E)]
        for banks, first in ((gates, H), (values, 0)):
            for e in range(E):
                picked = tokens[:].indirect(offsets[:, e * QC : (e + 1) * QC])
                nc.tensor.matmul(
                    banks[e][:, :Q],
                    weights[e][:, first : first + H],
                    picked,
                    start=True,
                    stop=True,
                )

        for e in range(E):
            opened = held.tile([H, Q], F32, name="opened%d" % e)
            nc.scalar.activation(opened[:], gates[e][:, :Q], SIGMOID)
            result = held.tile([H, Q], F32, name="result%d" % e, align_bytes=ROW)
            nc.vector.tensor_tensor(result[:], values[e][:, :Q], opened[:], MULT)
            nc.sync.dma_start(out[:, e * Q : (e + 1) * Q], result[:])
